import numpy as np
import ml_dtypes


def mxq(x, axis, fmt="e4m3"):
    dtype, down = {"e4m3": (ml_dtypes.float8_e4m3fn, 7), "e5m2": (ml_dtypes.float8_e5m2, 14)}[fmt]
    v = np.moveaxis(np.asarray(x, np.float32).astype(ml_dtypes.bfloat16).astype(np.float64), axis, -1)
    blocks = v.reshape(v.shape[:-1] + (-1, 32))
    amax = np.abs(blocks).max(-1, keepdims=True)
    byte = np.maximum(np.where(amax > 0, np.frexp(amax)[1] - 1 + 127, 0) - down, 1)
    scale = np.exp2(byte - 127.0)
    codes = (blocks / scale).astype(np.float32).astype(dtype).astype(np.float64)
    return np.moveaxis((codes * scale).reshape(v.shape), -1, axis)


WIDE = False


def mx_kscale(k, group=512):
    if not WIDE:
        return np.ones(k)
    levels = np.array([10, -10, 5, -5, 0])
    if group != 512:
        return np.exp2(np.random.permutation(np.resize(levels, k // group))).repeat(group)
    if k % 512:
        return np.exp2(np.random.permutation(np.resize(levels, k // 32))).repeat(32)
    a = np.empty((k // 512, 16))
    for p in range(k // 512):
        a[p, :8] = np.random.permutation(np.resize(levels, 8))
        for g in range(8):
            far = levels[np.abs(levels - a[p, g]) >= 10]
            a[p, g + 8] = far[np.random.randint(len(far))]
    return np.exp2(a.ravel()).repeat(32)


def f64(x):
    return np.asarray(x).astype(np.float64)


def striped(idx):
    return np.tile(np.asarray(idx).reshape(-1, 16).T, (8, 1)).astype(np.uint16)


def unstriped(offs):
    return offs[:16].T.reshape(-1).astype(np.int64)


H, KV, D, NQ, N = 2, 2, 256, 512, 512
CAP = 2.0


def setup_inputs():
    n = np.random.standard_normal
    s = mx_kscale(D, 0)[:, None]
    u = mx_kscale(N)
    t = np.random.uniform(0.5, 2.0, N) * u
    v = n((KV, N, 128))
    return {
        "qT": (n((H, D, NQ)) * s * (0.70 / np.sqrt(D))).astype(np.float32),
        "kT": (n((KV, D, N)) / s).astype(np.float32),
        "t": t.reshape(N, 1).astype(np.float32),
        "v": (v / t[:, None]).astype(np.float32),
        "mask": (np.arange(N)[:, None] <= np.sort(np.random.randint(N // 4, N, NQ))[None, :]).astype(np.float32),
        "og": n((H, NQ, 128)).astype(np.float32),
    }


def reference(qT, kT, t, v, mask, og):
    a = mxq(f64(kT), 1, "e4m3").transpose(0, 2, 1) @ mxq(f64(qT), 1, "e4m3")
    a = CAP * np.tanh(a / CAP)
    p = 1.0 / (1.0 + np.exp(-a))
    p = p * f64(mask)
    w = p * f64(t)
    y = mxq(w, 1, "e4m3").transpose(0, 2, 1) @ mxq(f64(v), 1, "e4m3")
    y = y / 16.0
    y = y / (1.0 + np.exp(-f64(og)))
    return y

@@ -1,0 +1,191 @@
+from contextlib import ExitStack
+
+import concourse.mybir as mybir
+
+H, D, NQ, N, E = 2, 256, 512, 512, 128
+FLOPS = 2 * H * N * NQ * D + 2 * H * NQ * N * E
+
+F32 = mybir.dt.float32
+BF16 = mybir.dt.bfloat16
+U32 = mybir.dt.uint32
+U8 = mybir.dt.uint8
+FP8X4 = mybir.dt.float8_e4m3fn_x4
+ACT = mybir.ActivationFunctionType
+MULT = mybir.AluOpType.mult
+
+P = 128
+PACK = 4
+ROWS = D // PACK
+QC = 128
+CHUNKS = NQ // QC
+RUN = 4
+K_VECTOR = 80
+SCORE_BANKS = 3
+
+
+def tile_rows_a_sigmoid_mask_cap_gate_kernel(tc, qT, kT, t, v, mask, og, out):
+    nc = tc.nc
+    with ExitStack() as ctx:
+        sb = ctx.enter_context(tc.tile_pool(name="sb", bufs=1))
+        ps = ctx.enter_context(tc.psum_pool(name="ps", bufs=1))
+        ctx.enter_context(tc.manual_schedule())
+
+        def sbuf(name, shape, dtype):
+            return sb.tile(shape, dtype, name=name, align_bytes=64)
+
+        def operand(name, width):
+            return (
+                sbuf(name + "_bf", [P, width * PACK], BF16),
+                sbuf(name + "_codes", [P, width], U32),
+                sbuf(name + "_scales", [P, width], U8),
+            )
+
+        def quantise(op, cols):
+            wide = slice(cols.start * PACK, cols.stop * PACK)
+            nc.vector.quantize_mx(out=op[1][:, cols].bitcast(FP8X4), scales=op[2][:, cols], in_=op[0][:, wide])
+
+        def matmul(acc, lhs, lhs_cols, rhs, rhs_cols, rows):
+            nc.tensor.matmul_mx(
+                out=acc,
+                lhsT=lhs[1][rows, lhs_cols].bitcast(FP8X4),
+                lhsT_scale=lhs[2][rows, lhs_cols],
+                rhs=rhs[1][rows, rhs_cols].bitcast(FP8X4),
+                rhs_scale=rhs[2][rows, rhs_cols],
+                start=True,
+                stop=True,
+            )
+
+        k_raw = sbuf("k_raw", [P, PACK, N], F32)
+        q_first = sbuf("q_first", [P, PACK, QC], F32)
+        q_rest = sbuf("q_rest", [P, PACK, NQ - QC], F32)
+        v_raw = sbuf("v_raw", [P, H, PACK, E], F32)
+        mask_raw = [sbuf("mask%d" % r, [P, NQ], F32) for r in range(PACK)]
+        og_raw = sbuf("og_raw", [P, H, CHUNKS, E], F32)
+        t_raw = sbuf("t_raw", [P, PACK], F32)
+        warm = sbuf("warm", [P, 2], F32)
+
+        q_hbm = qT.rearrange("h (p j) n -> (h p) j n", j=PACK)
+        mask_hbm = mask.rearrange("(s r) n -> s r n", r=PACK)
+        nc.sync.dma_start(out=k_raw[:], in_=kT.rearrange("h (p j) n -> (h p) j n", j=PACK))
+        nc.sync.dma_start(out=q_first[:], in_=q_hbm[:, :, 0:QC])
+        nc.sync.dma_start(out=q_rest[:], in_=q_hbm[:, :, QC:NQ])
+        nc.sync.dma_start(
+            out=v_raw[:].rearrange("s h r e -> s h (r e)"), in_=v.rearrange("h (s r) e -> s h (r e)", r=PACK)
+        )
+        for r in range(PACK):
+            nc.sync.dma_start(out=mask_raw[r][:], in_=mask_hbm[:, r, :])
+        nc.sync.dma_start(
+            out=og_raw[:].rearrange("m h c e -> m (h c) e"), in_=og.rearrange("h (c m) e -> m (h c) e", m=QC)
+        )
+        nc.gpsimd.dma_start(out=t_raw[:], in_=t.rearrange("(s r) one -> s (r one)", r=PACK))
+
+        nc.vector.memset(warm[:, 0:1], 0.0)
+        nc.scalar.activation(out=warm[:, 1:2], in_=warm[:, 0:1], func=ACT.Sigmoid)
+
+        k_op = operand("k", N)
+        q_ops = [operand("q_first", QC), operand("q_rest", NQ - QC)]
+        v_op = operand("v", H * E)
+        k_dst = k_op[0][:].rearrange("p (r s j) -> p s j r", r=PACK, j=PACK)
+        k_src = k_raw[:].rearrange("p j (s r) -> p s j r", r=PACK)
+        nc.vector.tensor_copy(out=k_dst[:, 0:K_VECTOR], in_=k_src[:, 0:K_VECTOR])
+        nc.scalar.copy(out=k_dst[:, K_VECTOR:P], in_=k_src[:, K_VECTOR:P])
+
+        def interleave_q(op, raw):
+            nc.vector.tensor_copy(
+                out=op[0][:].rearrange("p (c i j) -> p c j i", i=RUN, j=PACK),
+                in_=raw[:].rearrange("p j (c i) -> p c j i", i=RUN),
+            )
+
+        interleave_q(q_ops[0], q_first)
+        quantise(k_op, slice(0, N // 2))
+        quantise(q_ops[0], slice(0, QC))
+        quantise(k_op, slice(N // 2, N))
+
+        score = [[ps.tile([P, PACK, QC], F32, name="score%d_%d" % (h, b)) for b in range(SCORE_BANKS)] for h in range(H)]
+        y = [ps.tile([P, H, E], F32, name="y%d" % b) for b in range(2)]
+
+        def scores(c):
+            q_op = q_ops[min(c, 1)]
+            q_cols = slice(0, QC) if c == 0 else slice((c - 1) * QC, c * QC)
+            for half in range(2):
+                for h in range(H):
+                    for r in (2 * half, 2 * half + 1):
+                        rows = slice(h * ROWS, (h + 1) * ROWS)
+                        matmul(score[h][c % SCORE_BANKS][:, r, :], k_op, slice(r * P, (r + 1) * P), q_op, q_cols, rows)
+
+        capped = [[sbuf("capped%d_%d" % (c, h), [P, PACK * QC], F32) for h in range(H)] for c in range(CHUNKS)]
+        prob = [[sbuf("prob%d_%d" % (c, h), [P, PACK, QC], F32) for h in range(H)] for c in range(CHUNKS)]
+        w_ops = [[operand("w%d_%d" % (c, h), QC) for h in range(H)] for c in range(CHUNKS)]
+        mask_t = sbuf("mask_t", [P, PACK, NQ], F32)
+        gate = sbuf("gate", [P, H, CHUNKS, E], F32)
+        res = [sbuf("res%d" % c, [P, H, E], F32) for c in range(CHUNKS)]
+
+        def probabilities(c):
+            for h in range(H):
+                nc.scalar.activation(
+                    out=capped[c][h][:],
+                    in_=score[h][c % SCORE_BANKS][:].rearrange("s r n -> s (r n)"),
+                    func=ACT.Tanh,
+                    scale=0.5,
+                )
+            for h in range(H):
+                nc.scalar.activation(
+                    out=prob[c][h][:].rearrange("s r n -> s (r n)"), in_=capped[c][h][:], func=ACT.Sigmoid, scale=2.0
+                )
+
+        def gates(cs):
+            nc.scalar.activation(out=gate[:, :, cs, :], in_=og_raw[:, :, cs, :], func=ACT.Sigmoid)
+
+        def weights(c, h):
+            nc.vector.tensor_tensor(
+                out=w_ops[c][h][0][:].rearrange("s (g i r) -> s g r i", i=RUN, r=PACK),
+                in0=prob[c][h][:].rearrange("s r (g i) -> s g r i", i=RUN),
+                in1=mask_t[:, :, c * QC : (c + 1) * QC].rearrange("s r (g i) -> s g r i", i=RUN),
+                op=MULT,
+            )
+
+        def values(c, h):
+            quantise(w_ops[c][h], slice(0, QC))
+            matmul(y[c % 2][:, h, :], w_ops[c][h], slice(0, QC), v_op, slice(h * E, (h + 1) * E), slice(0, P))
+
+        def finish(c):
+            nc.vector.scalar_tensor_tensor(
+                out=res[c][:], in0=y[c % 2][:], scalar=1.0 / 16.0, in1=gate[:, :, c, :], op0=MULT, op1=MULT
+            )
+            nc.sync.dma_start(out=out[:, c * QC : (c + 1) * QC, :].rearrange("h m e -> m h e"), in_=res[c][:])
+
+        scores(0)
+        probabilities(0)
+
+        interleave_q(q_ops[1], q_rest)
+        quantise(q_ops[1], slice(0, QC))
+        quantise(q_ops[1], slice(QC, 3 * QC))
+        scores(1)
+        scores(2)
+        nc.vector.tensor_copy(
+            out=v_op[0][:].rearrange("s (h g i r) -> s h g r i", h=H, i=RUN, r=PACK),
+            in_=v_raw[:].rearrange("s h r (g i) -> s h g r i", i=RUN),
+        )
+        for r in range(PACK):
+            nc.vector.tensor_scalar(
+                out=mask_t[:, r, :], in0=mask_raw[r][:], scalar1=t_raw[:, r : r + 1], scalar2=None, op0=MULT
+            )
+            if r == 0:
+                quantise(v_op, slice(0, H * E))
+        probabilities(1)
+        scores(3)
+        gates(slice(0, 2))
+        probabilities(2)
+        probabilities(3)
+        gates(slice(2, 4))
+
+        steps = [(c, h) for c in range(CHUNKS) for h in range(H)]
+        for n, step in enumerate(steps):
+            weights(*step)
+            if n >= 1:
+                values(*steps[n - 1])
+            if n >= 4 and n % 2 == 0:
+                finish(n // 2 - 2)
+        finish(CHUNKS - 2)
+        values(*steps[-1])
+        finish(CHUNKS - 1)

@@ -59,7 +59,8 @@ def tile_rows_a_sigmoid_mask_cap_gate_kernel(tc, qT, kT, t, v, mask, og, out):
         q_first = sbuf("q_first", [P, PACK, QC], F32)
         q_rest = sbuf("q_rest", [P, PACK, NQ - QC], F32)
         v_raw = sbuf("v_raw", [P, H, PACK, E], F32)
-        mask_raw = [sbuf("mask%d" % r, [P, NQ], F32) for r in range(PACK)]
+        mask_places = [slice(0, 2), slice(2, 3), slice(3, 4)]
+        mask_raw = [sbuf("mask%d" % rs.start, [P, rs.stop - rs.start, NQ], F32) for rs in mask_places]
         og_raw = sbuf("og_raw", [P, H, CHUNKS, E], F32)
         t_raw = sbuf("t_raw", [P, PACK], F32)
         warm = sbuf("warm", [P, 2], F32)
@@ -69,34 +70,35 @@ def tile_rows_a_sigmoid_mask_cap_gate_kernel(tc, qT, kT, t, v, mask, og, out):
         nc.sync.dma_start(out=k_raw[:], in_=kT.rearrange("h (p j) n -> (h p) j n", j=PACK))
         nc.sync.dma_start(out=q_first[:], in_=q_hbm[:, :, 0:QC])
         nc.sync.dma_start(out=q_rest[:], in_=q_hbm[:, :, QC:NQ])
+        for rs, raw in zip(mask_places, mask_raw):
+            nc.sync.dma_start(out=raw[:], in_=mask_hbm[:, rs, :])
         nc.sync.dma_start(
             out=v_raw[:].rearrange("s h r e -> s h (r e)"), in_=v.rearrange("h (s r) e -> s h (r e)", r=PACK)
         )
-        for r in range(PACK):
-            nc.sync.dma_start(out=mask_raw[r][:], in_=mask_hbm[:, r, :])
         nc.sync.dma_start(
             out=og_raw[:].rearrange("m h c e -> m (h c) e"), in_=og.rearrange("h (c m) e -> m (h c) e", m=QC)
         )
-        nc.gpsimd.dma_start(out=t_raw[:], in_=t.rearrange("(s r) one -> s (r one)", r=PACK))
+        nc.scalar.dma_start(out=t_raw[:], in_=t.rearrange("(s r) one -> s (r one)", r=PACK))
 
         nc.vector.memset(warm[:, 0:1], 0.0)
         nc.scalar.activation(out=warm[:, 1:2], in_=warm[:, 0:1], func=ACT.Sigmoid)
 
         k_op = operand("k", N)
-        q_ops = [operand("q_first", QC), operand("q_rest", NQ - QC)]
+        q_ops = [operand("q%d" % c, QC) for c in range(CHUNKS)]
         v_op = operand("v", H * E)
         k_dst = k_op[0][:].rearrange("p (r s j) -> p s j r", r=PACK, j=PACK)
         k_src = k_raw[:].rearrange("p j (s r) -> p s j r", r=PACK)
         nc.vector.tensor_copy(out=k_dst[:, 0:K_VECTOR], in_=k_src[:, 0:K_VECTOR])
         nc.scalar.copy(out=k_dst[:, K_VECTOR:P], in_=k_src[:, K_VECTOR:P])
 
-        def interleave_q(op, raw):
+        def interleave_q(c):
+            raw = q_first[:] if c == 0 else q_rest[:, :, (c - 1) * QC : c * QC]
             nc.vector.tensor_copy(
-                out=op[0][:].rearrange("p (c i j) -> p c j i", i=RUN, j=PACK),
-                in_=raw[:].rearrange("p j (c i) -> p c j i", i=RUN),
+                out=q_ops[c][0][:].rearrange("p (g i j) -> p g j i", i=RUN, j=PACK),
+                in_=raw.rearrange("p j (g i) -> p g j i", i=RUN),
             )
 
-        interleave_q(q_ops[0], q_first)
+        interleave_q(0)
         quantise(k_op, slice(0, N // 2))
         quantise(q_ops[0], slice(0, QC))
         quantise(k_op, slice(N // 2, N))
@@ -104,16 +106,19 @@ def tile_rows_a_sigmoid_mask_cap_gate_kernel(tc, qT, kT, t, v, mask, og, out):
         score = [[ps.tile([P, PACK, QC], F32, name="score%d_%d" % (h, b)) for b in range(SCORE_BANKS)] for h in range(H)]
         y = [ps.tile([P, H, E], F32, name="y%d" % b) for b in range(2)]
 
-        def scores(c):
-            q_op = q_ops[min(c, 1)]
-            q_cols = slice(0, QC) if c == 0 else slice((c - 1) * QC, c * QC)
-            for half in range(2):
-                for h in range(H):
-                    for r in (2 * half, 2 * half + 1):
-                        rows = slice(h * ROWS, (h + 1) * ROWS)
-                        matmul(score[h][c % SCORE_BANKS][:, r, :], k_op, slice(r * P, (r + 1) * P), q_op, q_cols, rows)
+        def score_parts(c):
+            if c == 0:
+                return [(0, slice(0, 2)), (1, slice(2, 4))]
+            return [((c + 1) % SCORE_BANKS, slice(0, PACK))]
 
-        capped = [[sbuf("capped%d_%d" % (c, h), [P, PACK * QC], F32) for h in range(H)] for c in range(CHUNKS)]
+        def scores(c):
+            for bank, places in score_parts(c):
+                for h in range(H):
+                    for r in range(places.start, places.stop):
+                        rows = slice(h * ROWS, (h + 1) * ROWS)
+                        matmul(score[h][bank][:, r, :], k_op, slice(r * P, (r + 1) * P), q_ops[c], slice(0, QC), rows)
+
+        capped = [[sbuf("capped%d_%d" % (c, h), [P, PACK, QC], F32) for h in range(H)] for c in range(CHUNKS)]
         prob = [[sbuf("prob%d_%d" % (c, h), [P, PACK, QC], F32) for h in range(H)] for c in range(CHUNKS)]
         w_ops = [[operand("w%d_%d" % (c, h), QC) for h in range(H)] for c in range(CHUNKS)]
         mask_t = sbuf("mask_t", [P, PACK, NQ], F32)
@@ -121,17 +126,13 @@ def tile_rows_a_sigmoid_mask_cap_gate_kernel(tc, qT, kT, t, v, mask, og, out):
         res = [sbuf("res%d" % c, [P, H, E], F32) for c in range(CHUNKS)]
 
         def probabilities(c):
+            for bank, places in score_parts(c):
+                for h in range(H):
+                    nc.scalar.activation(
+                        out=capped[c][h][:, places, :], in_=score[h][bank][:, places, :], func=ACT.Tanh, scale=0.5
+                    )
             for h in range(H):
-                nc.scalar.activation(
-                    out=capped[c][h][:],
-                    in_=score[h][c % SCORE_BANKS][:].rearrange("s r n -> s (r n)"),
-                    func=ACT.Tanh,
-                    scale=0.5,
-                )
-            for h in range(H):
-                nc.scalar.activation(
-                    out=prob[c][h][:].rearrange("s r n -> s (r n)"), in_=capped[c][h][:], func=ACT.Sigmoid, scale=2.0
-                )
+                nc.scalar.activation(out=prob[c][h][:], in_=capped[c][h][:], func=ACT.Sigmoid, scale=2.0)
 
         def gates(cs):
             nc.scalar.activation(out=gate[:, :, cs, :], in_=og_raw[:, :, cs, :], func=ACT.Sigmoid)
@@ -148,44 +149,66 @@ def tile_rows_a_sigmoid_mask_cap_gate_kernel(tc, qT, kT, t, v, mask, og, out):
             quantise(w_ops[c][h], slice(0, QC))
             matmul(y[c % 2][:, h, :], w_ops[c][h], slice(0, QC), v_op, slice(h * E, (h + 1) * E), slice(0, P))
 
-        def finish(c):
+        def finish(c, heads):
             nc.vector.scalar_tensor_tensor(
-                out=res[c][:], in0=y[c % 2][:], scalar=1.0 / 16.0, in1=gate[:, :, c, :], op0=MULT, op1=MULT
+                out=res[c][:, heads, :],
+                in0=y[c % 2][:, heads, :],
+                scalar=1.0 / 16.0,
+                in1=gate[:, heads, c, :],
+                op0=MULT,
+                op1=MULT,
             )
-            nc.sync.dma_start(out=out[:, c * QC : (c + 1) * QC, :].rearrange("h m e -> m h e"), in_=res[c][:])
+            nc.sync.dma_start(
+                out=out[heads, c * QC : (c + 1) * QC, :].rearrange("h m e -> m h e"), in_=res[c][:, heads, :]
+            )
 
         scores(0)
         probabilities(0)
 
-        interleave_q(q_ops[1], q_rest)
+        interleave_q(1)
+        interleave_q(2)
         quantise(q_ops[1], slice(0, QC))
-        quantise(q_ops[1], slice(QC, 3 * QC))
         scores(1)
+        interleave_q(3)
+        quantise(q_ops[2], slice(0, QC))
         scores(2)
+        for rs, raw in zip(mask_places, mask_raw):
+            for r in range(rs.start, rs.stop):
+                nc.vector.tensor_scalar(
+                    out=mask_t[:, r, :], in0=raw[:, r - rs.start, :], scalar1=t_raw[:, r : r + 1], scalar2=None, op0=MULT
+                )
+                if r == 0:
+                    quantise(q_ops[3], slice(0, QC))
+        probabilities(1)
+        scores(3)
+        probabilities(2)
+        gates(slice(0, 2))
+        probabilities(3)
+        gates(slice(2, 4))
+
+        both = slice(0, H)
+        weights(0, 0)
+        weights(0, 1)
         nc.vector.tensor_copy(
             out=v_op[0][:].rearrange("s (h g i r) -> s h g r i", h=H, i=RUN, r=PACK),
             in_=v_raw[:].rearrange("s h r (g i) -> s h g r i", i=RUN),
         )
-        for r in range(PACK):
-            nc.vector.tensor_scalar(
-                out=mask_t[:, r, :], in0=mask_raw[r][:], scalar1=t_raw[:, r : r + 1], scalar2=None, op0=MULT
-            )
-            if r == 0:
-                quantise(v_op, slice(0, H * E))
-        probabilities(1)
-        scores(3)
-        gates(slice(0, 2))
-        probabilities(2)
-        probabilities(3)
-        gates(slice(2, 4))
-
-        steps = [(c, h) for c in range(CHUNKS) for h in range(H)]
-        for n, step in enumerate(steps):
-            weights(*step)
-            if n >= 1:
-                values(*steps[n - 1])
-            if n >= 4 and n % 2 == 0:
-                finish(n // 2 - 2)
-        finish(CHUNKS - 2)
-        values(*steps[-1])
-        finish(CHUNKS - 1)
+        weights(1, 0)
+        quantise(v_op, slice(0, H * E))
+        values(0, 0)
+        values(0, 1)
+        weights(1, 1)
+        values(1, 0)
+        weights(2, 0)
+        values(1, 1)
+        weights(2, 1)
+        finish(0, both)
+        values(2, 0)
+        values(2, 1)
+        weights(3, 0)
+        finish(1, both)
+        weights(3, 1)
+        values(3, 0)
+        values(3, 1)
+        finish(2, both)
+        finish(3, both)

@@ -18,9 +18,8 @@ PACK = 4
 ROWS = D // PACK
 QC = 128
 CHUNKS = NQ // QC
-RUN = 4
-K_VECTOR = 80
-SCORE_BANKS = 3
+RUN = 2
+SCORE_BANKS = 2
 
 
 def tile_rows_a_sigmoid_mask_cap_gate_kernel(tc, qT, kT, t, v, mask, og, out):
@@ -86,10 +85,10 @@ def tile_rows_a_sigmoid_mask_cap_gate_kernel(tc, qT, kT, t, v, mask, og, out):
         k_op = operand("k", N)
         q_ops = [operand("q%d" % c, QC) for c in range(CHUNKS)]
         v_op = operand("v", H * E)
-        k_dst = k_op[0][:].rearrange("p (r s j) -> p s j r", r=PACK, j=PACK)
-        k_src = k_raw[:].rearrange("p j (s r) -> p s j r", r=PACK)
-        nc.vector.tensor_copy(out=k_dst[:, 0:K_VECTOR], in_=k_src[:, 0:K_VECTOR])
-        nc.scalar.copy(out=k_dst[:, K_VECTOR:P], in_=k_src[:, K_VECTOR:P])
+        k_dst = k_op[0][:].rearrange("p (u r s j) -> p u s j r", r=RUN, s=P, j=PACK)
+        k_src = k_raw[:].rearrange("p j (s u r) -> p u s j r", r=RUN, s=P)
+        nc.vector.tensor_copy(out=k_dst[:, 0], in_=k_src[:, 0])
+        nc.scalar.copy(out=k_dst[:, 1], in_=k_src[:, 1])
 
         def interleave_q(c):
             raw = q_first[:] if c == 0 else q_rest[:, :, (c - 1) * QC : c * QC]
@@ -104,7 +103,10 @@ def tile_rows_a_sigmoid_mask_cap_gate_kernel(tc, qT, kT, t, v, mask, og, out):
         quantise(k_op, slice(N // 2, N))
 
         score = [[ps.tile([P, PACK, QC], F32, name="score%d_%d" % (h, b)) for b in range(SCORE_BANKS)] for h in range(H)]
-        y = [ps.tile([P, H, E], F32, name="y%d" % b) for b in range(2)]
+        y_banks = [ps.tile([P, H, E], F32, name="y%d" % b) for b in range(CHUNKS)]
+
+        def y(c, h):
+            return y_banks[0] if (c, h) == (CHUNKS - 1, H - 1) else y_banks[c]
 
         def score_parts(c):
             if c == 0:
@@ -125,6 +127,11 @@ def tile_rows_a_sigmoid_mask_cap_gate_kernel(tc, qT, kT, t, v, mask, og, out):
         gate = sbuf("gate", [P, H, CHUNKS, E], F32)
         res = [sbuf("res%d" % c, [P, H, E], F32) for c in range(CHUNKS)]
 
+        def query_parts(c, h):
+            if (c, h) == (CHUNKS - 1, H - 1):
+                return [slice(0, QC // 2), slice(QC // 2, QC)]
+            return [slice(0, QC)]
+
         def probabilities(c):
             for bank, places in score_parts(c):
                 for h in range(H):
@@ -132,27 +139,35 @@ def tile_rows_a_sigmoid_mask_cap_gate_kernel(tc, qT, kT, t, v, mask, og, out):
                         out=capped[c][h][:, places, :], in_=score[h][bank][:, places, :], func=ACT.Tanh, scale=0.5
                     )
             for h in range(H):
-                nc.scalar.activation(out=prob[c][h][:], in_=capped[c][h][:], func=ACT.Sigmoid, scale=2.0)
+                for qs in query_parts(c, h):
+                    nc.scalar.activation(
+                        out=prob[c][h][:, :, qs], in_=capped[c][h][:, :, qs], func=ACT.Sigmoid, scale=2.0
+                    )
 
         def gates(cs):
             nc.scalar.activation(out=gate[:, :, cs, :], in_=og_raw[:, :, cs, :], func=ACT.Sigmoid)
 
         def weights(c, h):
-            nc.vector.tensor_tensor(
-                out=w_ops[c][h][0][:].rearrange("s (g i r) -> s g r i", i=RUN, r=PACK),
-                in0=prob[c][h][:].rearrange("s r (g i) -> s g r i", i=RUN),
-                in1=mask_t[:, :, c * QC : (c + 1) * QC].rearrange("s r (g i) -> s g r i", i=RUN),
-                op=MULT,
-            )
+            for qs in query_parts(c, h):
+                nc.vector.tensor_tensor(
+                    out=w_ops[c][h][0][:, qs.start * PACK : qs.stop * PACK].rearrange(
+                        "s (g i r) -> s g r i", i=RUN, r=PACK
+                    ),
+                    in0=prob[c][h][:, :, qs].rearrange("s r (g i) -> s g r i", i=RUN),
+                    in1=mask_t[:, :, c * QC + qs.start : c * QC + qs.stop].rearrange("s r (g i) -> s g r i", i=RUN),
+                    op=MULT,
+                )
+
+        def quantise_w(c, h):
+            quantise(w_ops[c][h], slice(0, QC))
 
         def values(c, h):
-            quantise(w_ops[c][h], slice(0, QC))
-            matmul(y[c % 2][:, h, :], w_ops[c][h], slice(0, QC), v_op, slice(h * E, (h + 1) * E), slice(0, P))
+            matmul(y(c, h)[:, h, :], w_ops[c][h], slice(0, QC), v_op, slice(h * E, (h + 1) * E), slice(0, P))
 
         def finish(c, heads):
             nc.vector.scalar_tensor_tensor(
                 out=res[c][:, heads, :],
-                in0=y[c % 2][:, heads, :],
+                in0=y(c, heads.start)[:, heads, :],
                 scalar=1.0 / 16.0,
                 in1=gate[:, heads, c, :],
                 op0=MULT,
@@ -189,26 +204,33 @@ def tile_rows_a_sigmoid_mask_cap_gate_kernel(tc, qT, kT, t, v, mask, og, out):
         both = slice(0, H)
         weights(0, 0)
         weights(0, 1)
+        quantise_w(0, 0)
+        weights(1, 0)
+        quantise_w(0, 1)
         nc.vector.tensor_copy(
             out=v_op[0][:].rearrange("s (h g i r) -> s h g r i", h=H, i=RUN, r=PACK),
             in_=v_raw[:].rearrange("s h r (g i) -> s h g r i", i=RUN),
         )
-        weights(1, 0)
+        weights(1, 1)
         quantise(v_op, slice(0, H * E))
         values(0, 0)
         values(0, 1)
-        weights(1, 1)
+        quantise_w(1, 0)
         values(1, 0)
         weights(2, 0)
+        quantise_w(1, 1)
         values(1, 1)
         weights(2, 1)
         finish(0, both)
-        values(2, 0)
-        values(2, 1)
+        for h in range(H):
+            quantise_w(2, h)
+            values(2, h)
         weights(3, 0)
         finish(1, both)
         weights(3, 1)
-        values(3, 0)
-        values(3, 1)
+        for h in range(H):
+            quantise_w(3, h)
+            values(3, h)
         finish(2, both)
-        finish(3, both)
+        finish(3, slice(0, 1))
+        finish(3, slice(1, 2))

@@ -54,23 +54,23 @@ def tile_rows_a_sigmoid_mask_cap_gate_kernel(tc, qT, kT, t, v, mask, og, out):
                 stop=True,
             )
 
+        half = NQ // 2
         k_raw = sbuf("k_raw", [P, PACK, N], F32)
         q_first = sbuf("q_first", [P, PACK, QC], F32)
         q_rest = sbuf("q_rest", [P, PACK, NQ - QC], F32)
+        q_raw = [q_first[:], q_rest[:, :, 0:QC], q_rest[:, :, QC:]]
         v_raw = sbuf("v_raw", [P, H, PACK, E], F32)
-        mask_places = [slice(0, 2), slice(2, 3), slice(3, 4)]
-        mask_raw = [sbuf("mask%d" % rs.start, [P, rs.stop - rs.start, NQ], F32) for rs in mask_places]
+        mask_raw = [sbuf("mask%d" % u, [P, PACK, half], F32) for u in range(2)]
         og_raw = sbuf("og_raw", [P, H, CHUNKS, E], F32)
         t_raw = sbuf("t_raw", [P, PACK], F32)
-        warm = sbuf("warm", [P, 2], F32)
 
         q_hbm = qT.rearrange("h (p j) n -> (h p) j n", j=PACK)
         mask_hbm = mask.rearrange("(s r) n -> s r n", r=PACK)
         nc.sync.dma_start(out=k_raw[:], in_=kT.rearrange("h (p j) n -> (h p) j n", j=PACK))
         nc.sync.dma_start(out=q_first[:], in_=q_hbm[:, :, 0:QC])
         nc.sync.dma_start(out=q_rest[:], in_=q_hbm[:, :, QC:NQ])
-        for rs, raw in zip(mask_places, mask_raw):
-            nc.sync.dma_start(out=raw[:], in_=mask_hbm[:, rs, :])
+        nc.sync.dma_start(out=mask_raw[0][:], in_=mask_hbm[:, :, 0:half])
+        nc.sync.dma_start(out=mask_raw[1][:], in_=mask_hbm[:, :, half:NQ])
         nc.sync.dma_start(
             out=v_raw[:].rearrange("s h r e -> s h (r e)"), in_=v.rearrange("h (s r) e -> s h (r e)", r=PACK)
         )
@@ -79,22 +79,17 @@ def tile_rows_a_sigmoid_mask_cap_gate_kernel(tc, qT, kT, t, v, mask, og, out):
         )
         nc.scalar.dma_start(out=t_raw[:], in_=t.rearrange("(s r) one -> s (r one)", r=PACK))
 
-        nc.vector.memset(warm[:, 0:1], 0.0)
-        nc.scalar.activation(out=warm[:, 1:2], in_=warm[:, 0:1], func=ACT.Sigmoid)
-
         k_op = operand("k", N)
-        q_ops = [operand("q%d" % c, QC) for c in range(CHUNKS)]
+        q_ops = [operand("q0", QC), operand("q1", QC), operand("q2", half)]
         v_op = operand("v", H * E)
         k_dst = k_op[0][:].rearrange("p (u r s j) -> p u s j r", r=RUN, s=P, j=PACK)
         k_src = k_raw[:].rearrange("p j (s u r) -> p u s j r", r=RUN, s=P)
-        nc.vector.tensor_copy(out=k_dst[:, 0], in_=k_src[:, 0])
-        nc.scalar.copy(out=k_dst[:, 1], in_=k_src[:, 1])
+        nc.vector.tensor_copy(out=k_dst, in_=k_src)
 
         def interleave_q(c):
-            raw = q_first[:] if c == 0 else q_rest[:, :, (c - 1) * QC : c * QC]
             nc.vector.tensor_copy(
                 out=q_ops[c][0][:].rearrange("p (g i j) -> p g j i", i=RUN, j=PACK),
-                in_=raw.rearrange("p j (g i) -> p g j i", i=RUN),
+                in_=q_raw[c].rearrange("p j (g i) -> p g j i", i=RUN),
             )
 
         interleave_q(0)
@@ -114,16 +109,18 @@ def tile_rows_a_sigmoid_mask_cap_gate_kernel(tc, qT, kT, t, v, mask, og, out):
             return [((c + 1) % SCORE_BANKS, slice(0, PACK))]
 
         def scores(c):
+            q_op = q_ops[min(c, 2)]
+            q_cols = slice(max(c - 2, 0) * QC, (max(c - 2, 0) + 1) * QC)
             for bank, places in score_parts(c):
                 for h in range(H):
                     for r in range(places.start, places.stop):
                         rows = slice(h * ROWS, (h + 1) * ROWS)
-                        matmul(score[h][bank][:, r, :], k_op, slice(r * P, (r + 1) * P), q_ops[c], slice(0, QC), rows)
+                        matmul(score[h][bank][:, r, :], k_op, slice(r * P, (r + 1) * P), q_op, q_cols, rows)
 
         capped = [[sbuf("capped%d_%d" % (c, h), [P, PACK, QC], F32) for h in range(H)] for c in range(CHUNKS)]
         prob = [[sbuf("prob%d_%d" % (c, h), [P, PACK, QC], F32) for h in range(H)] for c in range(CHUNKS)]
-        w_ops = [[operand("w%d_%d" % (c, h), QC) for h in range(H)] for c in range(CHUNKS)]
-        mask_t = sbuf("mask_t", [P, PACK, NQ], F32)
+        w_ops = [operand("w%d" % c, H * QC) for c in range(CHUNKS)]
+        mask_t = [sbuf("mask_t%d" % u, [P, PACK, half], F32) for u in range(2)]
         gate = sbuf("gate", [P, H, CHUNKS, E], F32)
         res = [sbuf("res%d" % c, [P, H, E], F32) for c in range(CHUNKS)]
 
@@ -132,17 +129,25 @@ def tile_rows_a_sigmoid_mask_cap_gate_kernel(tc, qT, kT, t, v, mask, og, out):
                 return [slice(0, QC // 2), slice(QC // 2, QC)]
             return [slice(0, QC)]
 
-        def probabilities(c):
+        def caps(c, heads):
             for bank, places in score_parts(c):
-                for h in range(H):
+                for h in range(heads.start, heads.stop):
                     nc.scalar.activation(
-                        out=capped[c][h][:, places, :], in_=score[h][bank][:, places, :], func=ACT.Tanh, scale=0.5
+                        out=capped[c][h][:, places, :], in_=score[h][bank][:, places, :], func=ACT.Sigmoid
                     )
-            for h in range(H):
+
+        def probabilities(c, heads):
+            for h in range(heads.start, heads.stop):
                 for qs in query_parts(c, h):
                     nc.scalar.activation(
-                        out=prob[c][h][:, :, qs], in_=capped[c][h][:, :, qs], func=ACT.Sigmoid, scale=2.0
+                        out=prob[c][h][:, :, qs], in_=capped[c][h][:, :, qs], func=ACT.Sigmoid, scale=4.0, bias=-2.0
                     )
+
+        def scale_mask(u):
+            for r in range(PACK):
+                nc.vector.tensor_scalar(
+                    out=mask_t[u][:, r, :], in0=mask_raw[u][:, r, :], scalar1=t_raw[:, r : r + 1], scalar2=None, op0=MULT
+                )
 
         def gates(cs):
             nc.scalar.activation(out=gate[:, :, cs, :], in_=og_raw[:, :, cs, :], func=ACT.Sigmoid)
@@ -150,19 +155,21 @@ def tile_rows_a_sigmoid_mask_cap_gate_kernel(tc, qT, kT, t, v, mask, og, out):
         def weights(c, h):
             for qs in query_parts(c, h):
                 nc.vector.tensor_tensor(
-                    out=w_ops[c][h][0][:, qs.start * PACK : qs.stop * PACK].rearrange(
+                    out=w_ops[c][0][:, (h * QC + qs.start) * PACK : (h * QC + qs.stop) * PACK].rearrange(
                         "s (g i r) -> s g r i", i=RUN, r=PACK
                     ),
                     in0=prob[c][h][:, :, qs].rearrange("s r (g i) -> s g r i", i=RUN),
-                    in1=mask_t[:, :, c * QC + qs.start : c * QC + qs.stop].rearrange("s r (g i) -> s g r i", i=RUN),
+                    in1=mask_t[c // 2][:, :, c % 2 * QC + qs.start : c % 2 * QC + qs.stop].rearrange(
+                        "s r (g i) -> s g r i", i=RUN
+                    ),
                     op=MULT,
                 )
 
-        def quantise_w(c, h):
-            quantise(w_ops[c][h], slice(0, QC))
+        def quantise_w(c, heads):
+            quantise(w_ops[c], slice(heads.start * QC, heads.stop * QC))
 
         def values(c, h):
-            matmul(y(c, h)[:, h, :], w_ops[c][h], slice(0, QC), v_op, slice(h * E, (h + 1) * E), slice(0, P))
+            matmul(y(c, h)[:, h, :], w_ops[c], slice(h * QC, (h + 1) * QC), v_op, slice(h * E, (h + 1) * E), slice(0, P))
 
         def finish(c, heads):
             nc.vector.scalar_tensor_tensor(
@@ -177,36 +184,35 @@ def tile_rows_a_sigmoid_mask_cap_gate_kernel(tc, qT, kT, t, v, mask, og, out):
                 out=out[heads, c * QC : (c + 1) * QC, :].rearrange("h m e -> m h e"), in_=res[c][:, heads, :]
             )
 
+        both, first, second = slice(0, H), slice(0, 1), slice(1, 2)
         scores(0)
-        probabilities(0)
-
+        caps(0, both)
+        probabilities(0, both)
         interleave_q(1)
         interleave_q(2)
         quantise(q_ops[1], slice(0, QC))
+        quantise(q_ops[2], slice(0, half))
         scores(1)
-        interleave_q(3)
-        quantise(q_ops[2], slice(0, QC))
+        caps(1, both)
+        probabilities(1, both)
         scores(2)
-        for rs, raw in zip(mask_places, mask_raw):
-            for r in range(rs.start, rs.stop):
-                nc.vector.tensor_scalar(
-                    out=mask_t[:, r, :], in0=raw[:, r - rs.start, :], scalar1=t_raw[:, r : r + 1], scalar2=None, op0=MULT
-                )
-                if r == 0:
-                    quantise(q_ops[3], slice(0, QC))
-        probabilities(1)
         scores(3)
-        probabilities(2)
-        gates(slice(0, 2))
-        probabilities(3)
-        gates(slice(2, 4))
-
-        both = slice(0, H)
+        caps(2, both)
+        probabilities(2, first)
+        caps(3, first)
+        probabilities(2, second)
+        probabilities(3, first)
+        caps(3, second)
+        gates(slice(0, 1))
+        probabilities(3, second)
+        for c in range(1, CHUNKS):
+            gates(slice(c, c + 1))
+        scale_mask(0)
         weights(0, 0)
         weights(0, 1)
-        quantise_w(0, 0)
+        scale_mask(1)
+        quantise_w(0, both)
         weights(1, 0)
-        quantise_w(0, 1)
         nc.vector.tensor_copy(
             out=v_op[0][:].rearrange("s (h g i r) -> s h g r i", h=H, i=RUN, r=PACK),
             in_=v_raw[:].rearrange("s h r (g i) -> s h g r i", i=RUN),
@@ -215,22 +221,22 @@ def tile_rows_a_sigmoid_mask_cap_gate_kernel(tc, qT, kT, t, v, mask, og, out):
         quantise(v_op, slice(0, H * E))
         values(0, 0)
         values(0, 1)
-        quantise_w(1, 0)
-        values(1, 0)
         weights(2, 0)
-        quantise_w(1, 1)
+        quantise_w(1, both)
+        values(1, 0)
         values(1, 1)
         weights(2, 1)
-        finish(0, both)
-        for h in range(H):
-            quantise_w(2, h)
-            values(2, h)
         weights(3, 0)
-        finish(1, both)
+        quantise_w(2, both)
+        values(2, 0)
+        values(2, 1)
+        quantise_w(3, first)
+        values(3, 0)
         weights(3, 1)
-        for h in range(H):
-            quantise_w(3, h)
-            values(3, h)
+        finish(0, both)
+        quantise_w(3, second)
+        values(3, 1)
+        finish(1, both)
         finish(2, both)
-        finish(3, slice(0, 1))
-        finish(3, slice(1, 2))
+        finish(3, first)
+        finish(3, second)

@@ -55,7 +55,7 @@ def tile_rows_a_sigmoid_mask_cap_gate_kernel(tc, qT, kT, t, v, mask, og, out):
             )
 
         half = NQ // 2
-        k_raw = sbuf("k_raw", [P, PACK, N], F32)
+        k_raw = [sbuf("k_raw%d" % w, [P, 2, N], F32) for w in range(2)]
         q_first = sbuf("q_first", [P, PACK, QC], F32)
         q_rest = sbuf("q_rest", [P, PACK, NQ - QC], F32)
         q_raw = [q_first[:], q_rest[:, :, 0:QC], q_rest[:, :, QC:]]
@@ -66,9 +66,12 @@ def tile_rows_a_sigmoid_mask_cap_gate_kernel(tc, qT, kT, t, v, mask, og, out):
 
         q_hbm = qT.rearrange("h (p j) n -> (h p) j n", j=PACK)
         mask_hbm = mask.rearrange("(s r) n -> s r n", r=PACK)
-        nc.sync.dma_start(out=k_raw[:], in_=kT.rearrange("h (p j) n -> (h p) j n", j=PACK))
+        k_hbm = kT.rearrange("h (p j) n -> (h p) j n", j=PACK)
+        for w in range(2):
+            nc.sync.dma_start(out=k_raw[w][:], in_=k_hbm[:, 2 * w : 2 * w + 2, :])
         nc.sync.dma_start(out=q_first[:], in_=q_hbm[:, :, 0:QC])
         nc.sync.dma_start(out=q_rest[:], in_=q_hbm[:, :, QC:NQ])
+        nc.sync.dma_start(out=t_raw[:], in_=t.rearrange("(s r) one -> s (r one)", r=PACK))
         nc.sync.dma_start(out=mask_raw[0][:], in_=mask_hbm[:, :, 0:half])
         nc.sync.dma_start(out=mask_raw[1][:], in_=mask_hbm[:, :, half:NQ])
         nc.sync.dma_start(
@@ -77,14 +80,13 @@ def tile_rows_a_sigmoid_mask_cap_gate_kernel(tc, qT, kT, t, v, mask, og, out):
         nc.sync.dma_start(
             out=og_raw[:].rearrange("m h c e -> m (h c) e"), in_=og.rearrange("h (c m) e -> m (h c) e", m=QC)
         )
-        nc.scalar.dma_start(out=t_raw[:], in_=t.rearrange("(s r) one -> s (r one)", r=PACK))
 
         k_op = operand("k", N)
         q_ops = [operand("q0", QC), operand("q1", QC), operand("q2", half)]
         v_op = operand("v", H * E)
-        k_dst = k_op[0][:].rearrange("p (u r s j) -> p u s j r", r=RUN, s=P, j=PACK)
-        k_src = k_raw[:].rearrange("p j (s u r) -> p u s j r", r=RUN, s=P)
-        nc.vector.tensor_copy(out=k_dst, in_=k_src)
+        k_dst = k_op[0][:].rearrange("p (u r s w j) -> p w u s j r", r=RUN, s=P, w=2, j=2)
+        for w in range(2):
+            nc.vector.tensor_copy(out=k_dst[:, w], in_=k_raw[w][:].rearrange("p j (s u r) -> p u s j r", r=RUN, s=P))
 
         def interleave_q(c):
             nc.vector.tensor_copy(

from contextlib import ExitStack

import concourse.mybir as mybir

H, D, NQ, N, E = 2, 256, 512, 512, 128
FLOPS = 2 * H * N * NQ * D + 2 * H * NQ * N * E

F32 = mybir.dt.float32
BF16 = mybir.dt.bfloat16
U32 = mybir.dt.uint32
U8 = mybir.dt.uint8
FP8X4 = mybir.dt.float8_e4m3fn_x4
ACT = mybir.ActivationFunctionType
MULT = mybir.AluOpType.mult

P = 128
PACK = 4
ROWS = D // PACK
QC = 128
CHUNKS = NQ // QC
RUN = 2
SCORE_BANKS = 2


def tile_rows_a_sigmoid_mask_cap_gate_kernel(tc, qT, kT, t, v, mask, og, out):
    nc = tc.nc
    with ExitStack() as ctx:
        sb = ctx.enter_context(tc.tile_pool(name="sb", bufs=1))
        ps = ctx.enter_context(tc.psum_pool(name="ps", bufs=1))
        ctx.enter_context(tc.manual_schedule())

        def sbuf(name, shape, dtype):
            return sb.tile(shape, dtype, name=name, align_bytes=64)

        def operand(name, width):
            return (
                sbuf(name + "_bf", [P, width * PACK], BF16),
                sbuf(name + "_codes", [P, width], U32),
                sbuf(name + "_scales", [P, width], U8),
            )

        def quantise(op, cols):
            wide = slice(cols.start * PACK, cols.stop * PACK)
            nc.vector.quantize_mx(out=op[1][:, cols].bitcast(FP8X4), scales=op[2][:, cols], in_=op[0][:, wide])

        def matmul(acc, lhs, lhs_cols, rhs, rhs_cols, rows):
            nc.tensor.matmul_mx(
                out=acc,
                lhsT=lhs[1][rows, lhs_cols].bitcast(FP8X4),
                lhsT_scale=lhs[2][rows, lhs_cols],
                rhs=rhs[1][rows, rhs_cols].bitcast(FP8X4),
                rhs_scale=rhs[2][rows, rhs_cols],
                start=True,
                stop=True,
            )

        half = NQ // 2
        k_raw = [sbuf("k_raw%d" % w, [P, 2, N], F32) for w in range(2)]
        q_first = sbuf("q_first", [P, PACK, QC], F32)
        q_rest = sbuf("q_rest", [P, PACK, NQ - QC], F32)
        q_raw = [q_first[:], q_rest[:, :, 0:QC], q_rest[:, :, QC:]]
        v_raw = sbuf("v_raw", [P, H, PACK, E], F32)
        mask_raw = [sbuf("mask%d" % u, [P, PACK, half], F32) for u in range(2)]
        og_raw = sbuf("og_raw", [P, H, CHUNKS, E], F32)
        t_raw = sbuf("t_raw", [P, PACK], F32)

        q_hbm = qT.rearrange("h (p j) n -> (h p) j n", j=PACK)
        mask_hbm = mask.rearrange("(s r) n -> s r n", r=PACK)
        k_hbm = kT.rearrange("h (p j) n -> (h p) j n", j=PACK)
        for w in range(2):
            nc.sync.dma_start(out=k_raw[w][:], in_=k_hbm[:, 2 * w : 2 * w + 2, :])
        nc.sync.dma_start(out=q_first[:], in_=q_hbm[:, :, 0:QC])
        nc.sync.dma_start(out=q_rest[:], in_=q_hbm[:, :, QC:NQ])
        nc.sync.dma_start(out=t_raw[:], in_=t.rearrange("(s r) one -> s (r one)", r=PACK))
        nc.sync.dma_start(out=mask_raw[0][:], in_=mask_hbm[:, :, 0:half])
        nc.sync.dma_start(out=mask_raw[1][:], in_=mask_hbm[:, :, half:NQ])
        nc.sync.dma_start(
            out=v_raw[:].rearrange("s h r e -> s h (r e)"), in_=v.rearrange("h (s r) e -> s h (r e)", r=PACK)
        )
        nc.sync.dma_start(
            out=og_raw[:].rearrange("m h c e -> m (h c) e"), in_=og.rearrange("h (c m) e -> m (h c) e", m=QC)
        )

        k_op = operand("k", N)
        q_ops = [operand("q0", QC), operand("q1", QC), operand("q2", half)]
        v_op = operand("v", H * E)
        k_dst = k_op[0][:].rearrange("p (u r s w j) -> p w u s j r", r=RUN, s=P, w=2, j=2)
        for w in range(2):
            nc.vector.tensor_copy(out=k_dst[:, w], in_=k_raw[w][:].rearrange("p j (s u r) -> p u s j r", r=RUN, s=P))

        def interleave_q(c):
            nc.vector.tensor_copy(
                out=q_ops[c][0][:].rearrange("p (g i j) -> p g j i", i=RUN, j=PACK),
                in_=q_raw[c].rearrange("p j (g i) -> p g j i", i=RUN),
            )

        interleave_q(0)
        quantise(k_op, slice(0, N // 2))
        quantise(q_ops[0], slice(0, QC))
        quantise(k_op, slice(N // 2, N))

        score = [[ps.tile([P, PACK, QC], F32, name="score%d_%d" % (h, b)) for b in range(SCORE_BANKS)] for h in range(H)]
        y_banks = [ps.tile([P, H, E], F32, name="y%d" % b) for b in range(CHUNKS)]

        def y(c, h):
            return y_banks[0] if (c, h) == (CHUNKS - 1, H - 1) else y_banks[c]

        def score_parts(c):
            if c == 0:
                return [(0, slice(0, 2)), (1, slice(2, 4))]
            return [((c + 1) % SCORE_BANKS, slice(0, PACK))]

        def scores(c):
            q_op = q_ops[min(c, 2)]
            q_cols = slice(max(c - 2, 0) * QC, (max(c - 2, 0) + 1) * QC)
            for bank, places in score_parts(c):
                for h in range(H):
                    for r in range(places.start, places.stop):
                        rows = slice(h * ROWS, (h + 1) * ROWS)
                        matmul(score[h][bank][:, r, :], k_op, slice(r * P, (r + 1) * P), q_op, q_cols, rows)

        capped = [[sbuf("capped%d_%d" % (c, h), [P, PACK, QC], F32) for h in range(H)] for c in range(CHUNKS)]
        prob = [[sbuf("prob%d_%d" % (c, h), [P, PACK, QC], F32) for h in range(H)] for c in range(CHUNKS)]
        w_ops = [operand("w%d" % c, H * QC) for c in range(CHUNKS)]
        mask_t = [sbuf("mask_t%d" % u, [P, PACK, half], F32) for u in range(2)]
        gate = sbuf("gate", [P, H, CHUNKS, E], F32)
        res = [sbuf("res%d" % c, [P, H, E], F32) for c in range(CHUNKS)]

        def query_parts(c, h):
            if (c, h) == (CHUNKS - 1, H - 1):
                return [slice(0, QC // 2), slice(QC // 2, QC)]
            return [slice(0, QC)]

        def caps(c, heads):
            for bank, places in score_parts(c):
                for h in range(heads.start, heads.stop):
                    nc.scalar.activation(
                        out=capped[c][h][:, places, :], in_=score[h][bank][:, places, :], func=ACT.Sigmoid
                    )

        def probabilities(c, heads):
            for h in range(heads.start, heads.stop):
                for qs in query_parts(c, h):
                    nc.scalar.activation(
                        out=prob[c][h][:, :, qs], in_=capped[c][h][:, :, qs], func=ACT.Sigmoid, scale=4.0, bias=-2.0
                    )

        def scale_mask(u):
            for r in range(PACK):
                nc.vector.tensor_scalar(
                    out=mask_t[u][:, r, :], in0=mask_raw[u][:, r, :], scalar1=t_raw[:, r : r + 1], scalar2=None, op0=MULT
                )

        def gates(cs):
            nc.scalar.activation(out=gate[:, :, cs, :], in_=og_raw[:, :, cs, :], func=ACT.Sigmoid)

        def weights(c, h):
            for qs in query_parts(c, h):
                nc.vector.tensor_tensor(
                    out=w_ops[c][0][:, (h * QC + qs.start) * PACK : (h * QC + qs.stop) * PACK].rearrange(
                        "s (g i r) -> s g r i", i=RUN, r=PACK
                    ),
                    in0=prob[c][h][:, :, qs].rearrange("s r (g i) -> s g r i", i=RUN),
                    in1=mask_t[c // 2][:, :, c % 2 * QC + qs.start : c % 2 * QC + qs.stop].rearrange(
                        "s r (g i) -> s g r i", i=RUN
                    ),
                    op=MULT,
                )

        def quantise_w(c, heads):
            quantise(w_ops[c], slice(heads.start * QC, heads.stop * QC))

        def values(c, h):
            matmul(y(c, h)[:, h, :], w_ops[c], slice(h * QC, (h + 1) * QC), v_op, slice(h * E, (h + 1) * E), slice(0, P))

        def finish(c, heads):
            nc.vector.scalar_tensor_tensor(
                out=res[c][:, heads, :],
                in0=y(c, heads.start)[:, heads, :],
                scalar=1.0 / 16.0,
                in1=gate[:, heads, c, :],
                op0=MULT,
                op1=MULT,
            )
            nc.sync.dma_start(
                out=out[heads, c * QC : (c + 1) * QC, :].rearrange("h m e -> m h e"), in_=res[c][:, heads, :]
            )

        both, first, second = slice(0, H), slice(0, 1), slice(1, 2)
        scores(0)
        caps(0, both)
        probabilities(0, both)
        interleave_q(1)
        interleave_q(2)
        quantise(q_ops[1], slice(0, QC))
        quantise(q_ops[2], slice(0, half))
        scores(1)
        caps(1, both)
        probabilities(1, both)
        scores(2)
        scores(3)
        caps(2, both)
        probabilities(2, first)
        caps(3, first)
        probabilities(2, second)
        probabilities(3, first)
        caps(3, second)
        gates(slice(0, 1))
        probabilities(3, second)
        for c in range(1, CHUNKS):
            gates(slice(c, c + 1))
        scale_mask(0)
        weights(0, 0)
        weights(0, 1)
        scale_mask(1)
        quantise_w(0, both)
        weights(1, 0)
        nc.vector.tensor_copy(
            out=v_op[0][:].rearrange("s (h g i r) -> s h g r i", h=H, i=RUN, r=PACK),
            in_=v_raw[:].rearrange("s h r (g i) -> s h g r i", i=RUN),
        )
        weights(1, 1)
        quantise(v_op, slice(0, H * E))
        values(0, 0)
        values(0, 1)
        weights(2, 0)
        quantise_w(1, both)
        values(1, 0)
        values(1, 1)
        weights(2, 1)
        weights(3, 0)
        quantise_w(2, both)
        values(2, 0)
        values(2, 1)
        quantise_w(3, first)
        values(3, 0)
        weights(3, 1)
        finish(0, both)
        quantise_w(3, second)
        values(3, 1)
        finish(1, both)
        finish(2, both)
        finish(3, first)
        finish(3, second)
